import numpy as np, ml_dtypes
CORES = [16,17,18,19,150,151]
N = 6
W, KW, DIL = 256, 3, 2
H = (KW // 2) * DIL
def setup_inputs(rng):
    return {"x": rng.standard_normal((N, 128, W), dtype=np.float32).astype(ml_dtypes.bfloat16), "w": rng.standard_normal((N, 128, KW * 128), dtype=np.float32).astype(ml_dtypes.bfloat16)}
def setup_inputs_big(rng):
    d = setup_inputs(rng)
    for k in ("x", "w"): d[k] = (d[k].astype(np.float32) * 1024.0).astype(d[k].dtype)
    return d
def setup_inputs_small(rng):
    d = setup_inputs(rng)
    for k in ("x", "w"): d[k] = (d[k].astype(np.float32) * (1 / 1024.0)).astype(d[k].dtype)
    return d
def reference(x, w):
    X, W_ = x.astype(np.float64), w.astype(np.float64)
    g = np.concatenate(list(X), axis=1)
    p = np.pad(g, ((0, 0), (H, H)))
    y = np.zeros((N, 128, W))
    for r in range(N):
        for i in range(KW):
            y[r] += W_[r][:, 128 * i:128 * i + 128].T @ p[:, W * r + i * DIL:W * r + i * DIL + W]
    return {"y": y.astype(ml_dtypes.bfloat16 if x.dtype != np.float64 else np.float64)}

from concourse.bass import DstId, RemoteDMATransfer

CH, WID, TAPS, HALO = 128, 256, 3, 2
ENGINES_A_SEND = 4

SCRATCH = {
    "xs": ("sbuf", [CH, WID], "bfloat16"),
    "ws": ("sbuf", [CH, TAPS * CH], "bfloat16"),
    "hl": ("sbuf", [CH, HALO], "bfloat16"),
    "hr": ("sbuf", [CH, HALO], "bfloat16"),
    "ys": ("sbuf", [CH, WID], "bfloat16"),
    "pin": ("psum", [CH, 512], "float32"),
    "pl": ("psum", [CH, 512], "float32"),
    "pr": ("psum", [CH, 512], "float32"),
}
SEMAPHORES = ["x_in", "w_in", "got_l", "got_r", "sent", "mm_in", "mm_l", "mm_r", "rounded", "stored"]


def _pick(allowed, count, taken):
    m = 0
    for b in range(allowed.bit_length()):
        if count and (allowed >> b) & 1 and not (taken >> b) & 1:
            m |= 1 << b
            count -= 1
    return m


def rank_program(g, core, T, topo):
    rank = T.rank_of(core)
    if rank is None:
        return
    n = len(T.cores)
    S = T.sem
    left = T.cores[rank - 1] if rank > 0 else None
    right = T.cores[rank + 1] if rank < n - 1 else None

    g.sync.dma_start(T.xs[:, :], T.x[:, :]).then_inc(S.x_in, 16)
    g.scalar.dma_start(T.ws[:, :], T.w[:, :]).then_inc(S.w_in, 16)

    sends = []
    if left is not None:
        sends.append((left, T.xs[:, 0:HALO], T.hr[:, :], S.got_r))
    if right is not None:
        sends.append((right, T.xs[:, WID - HALO:WID], T.hl[:, :], S.got_l))
    sends.sort(key=lambda s: bin(topo.mask(core, s[0])).count("1"))
    taken, transfers = 0, []
    for dst, src_ap, dst_ap, sem in sends:
        rid, pid = topo.addr(dst, core)
        m = _pick(topo.mask(core, dst), ENGINES_A_SEND, taken)
        taken |= m
        transfers.append(RemoteDMATransfer(dst_ids=[DstId(rid=rid, pnc=pid)], dma_engine_mask=m, remote_sem=sem,
                                           src=src_ap, dst=dst_ap))
    g.wait_ge(S.x_in, 16)
    g.remote_dma_fused(transfers, local_sem=S.sent)

    def tap(i):
        return T.ws[:, CH * i:CH * (i + 1)]

    te, ve = g.tensor, g.vector
    inner = WID - 2 * HALO
    te.wait_ge(S.x_in, 16)
    te.wait_ge(S.w_in, 16)
    te.matmul(T.pin[:, 0:inner], tap(1), T.xs[:, HALO:HALO + inner], True, False)
    te.matmul(T.pin[:, 0:inner], tap(0), T.xs[:, 0:inner], False, False)
    te.matmul(T.pin[:, 0:inner], tap(2), T.xs[:, 2 * HALO:2 * HALO + inner], False, True).then_inc(S.mm_in, 1)

    sides = [
        (left, T.pl, 0, 2, HALO, 0, T.hl, S.got_l, S.mm_l, 0),
        (right, T.pr, WID - HALO, 0, WID - 2 * HALO, 2, T.hr, S.got_r, S.mm_r, WID - HALO),
    ]

    def distance(side):
        nb = side[0]
        if nb is None:
            return 0
        return 1 if (topo.host(nb), topo.chip(nb)) == (topo.host(core), topo.chip(core)) else 2

    sides.sort(key=distance)
    for nb, bank, c_mid, own_tap, c_own, _, _, _, done, _ in sides:
        te.matmul(bank[:, 0:HALO], tap(1), T.xs[:, c_mid:c_mid + HALO], True, False)
        last = te.matmul(bank[:, 0:HALO], tap(own_tap), T.xs[:, c_own:c_own + HALO], False, nb is None)
        if nb is None:
            last.then_inc(done, 1)
    for nb, bank, _, _, _, halo_tap, halo, got, done, _ in sides:
        if nb is not None:
            te.wait_ge(got, ENGINES_A_SEND)
            te.matmul(bank[:, 0:HALO], tap(halo_tap), halo[:, :], False, True).then_inc(done, 1)

    ve.wait_ge(S.mm_in, 1)
    ve.tensor_copy(T.ys[:, HALO:HALO + inner], T.pin[:, 0:inner]).then_inc(S.rounded, 1)
    for _, bank, _, _, _, _, _, _, done, c_y in sides:
        ve.wait_ge(done, 1)
        ve.tensor_copy(T.ys[:, c_y:c_y + HALO], bank[:, 0:HALO]).then_inc(S.rounded, 1)

    g.sync.wait_ge(S.rounded, 3)
    g.sync.dma_start(T.y[:, :], T.ys[:, :]).then_inc(S.stored, 16)
    g.sync.wait_ge(S.stored, 16)
    g.wait_ge(S.sent, ENGINES_A_SEND * len(transfers))
